import numpy as np
import ml_dtypes


def mxq(x, axis, fmt="e4m3"):
    dtype, down = {"e4m3": (ml_dtypes.float8_e4m3fn, 7), "e5m2": (ml_dtypes.float8_e5m2, 14)}[fmt]
    v = np.moveaxis(np.asarray(x, np.float32).astype(ml_dtypes.bfloat16).astype(np.float64), axis, -1)
    blocks = v.reshape(v.shape[:-1] + (-1, 32))
    amax = np.abs(blocks).max(-1, keepdims=True)
    byte = np.maximum(np.where(amax > 0, np.frexp(amax)[1] - 1 + 127, 0) - down, 1)
    scale = np.exp2(byte - 127.0)
    codes = (blocks / scale).astype(np.float32).astype(dtype).astype(np.float64)
    return np.moveaxis((codes * scale).reshape(v.shape), -1, axis)


WIDE = False


def mx_kscale(k):
    if not WIDE:
        return np.ones(k)
    levels = np.array([10, -10, 5, -5, 0])
    if k % 512:
        return np.exp2(np.random.permutation(np.resize(levels, k // 32))).repeat(32)
    a = np.empty((k // 512, 16))
    for p in range(k // 512):
        a[p, :8] = np.random.permutation(np.resize(levels, 8))
        for g in range(8):
            far = levels[np.abs(levels - a[p, g]) >= 10]
            a[p, g + 8] = far[np.random.randint(len(far))]
    return np.exp2(a.ravel()).repeat(32)


BF16 = ml_dtypes.bfloat16


def bf(x):
    return np.asarray(x, np.float32).astype(BF16)


def f64(x):
    return np.asarray(x).astype(np.float64)


B, L, D, R = 4, 384, 1024, 1024

SLOPE = 0.1


def leaky(z):
    return np.maximum(z, SLOPE * z)


def draw0():
    s, t = mx_kscale(D), mx_kscale(R)
    return {"x": bf(np.random.standard_normal((B * L, D)) * s),
            "w_dep": bf(np.random.standard_normal((D, R)) / np.sqrt(D) / s[:, None] * t),
            "b_dep": bf(0.3 * np.random.standard_normal(R) * t),
            "w_head": bf(np.random.standard_normal((D, R)) / np.sqrt(D) / s[:, None] / t),
            "b_head": bf(0.3 * np.random.standard_normal(R) / t),
            "u": bf(np.random.standard_normal(R)),
            "v": bf(0.3 * np.random.standard_normal(R) * t),
            "pos": bf(0.3 * np.random.standard_normal((L, L)))}


def core(x, w_dep, b_dep, w_head, b_head, u, v, pos):
    xq = mxq(f64(x), 1, "e4m3")
    dep = leaky((xq @ mxq(f64(w_dep), 0, "e4m3")) + f64(b_dep))
    head = leaky((xq @ mxq(f64(w_head), 0, "e4m3")) + f64(b_head))
    query = dep * f64(u) + f64(v)
    qq = mxq(query, 1, "e4m3").reshape(B, L, R)
    hq = mxq(head, 1, "e4m3").reshape(B, L, R)
    scores = (qq @ hq.swapaxes(1, 2)) / np.sqrt(R) + f64(pos)
    e = np.exp(scores - np.max(scores, axis=2, keepdims=True))
    lift = L * e / np.sum(e, axis=2, keepdims=True)
    return scores, lift


def e4m3fn_bytes(y):
    return np.clip(np.asarray(y, np.float64), -448.0, 448.0).astype(np.float32).astype(ml_dtypes.float8_e4m3fn).view(np.uint8)


def e4m3fn_values(b):
    return np.asarray(b, np.uint8).view(ml_dtypes.float8_e4m3fn).astype(np.float64)


def setup_inputs():
    d = draw0()
    x0 = np.asarray(d['x']).astype(np.float64)
    s = (np.max(np.abs(x0), axis=(0,), keepdims=True) / 448.0).astype(np.float32)
    out = {}
    for k, v in d.items():
        if k == 'x':
            out['x_bytes'] = e4m3fn_bytes(x0 / s.astype(np.float64))
            out['x_scale'] = s
        else:
            out[k] = v
    return out


def reference(x_bytes, x_scale, w_dep, b_dep, w_head, b_head, u, v, pos):
    return core(e4m3fn_values(x_bytes) * x_scale.astype(np.float64), w_dep, b_dep, w_head, b_head, u, v, pos)

@@ -1,0 +1,338 @@
+from contextlib import ExitStack
+
+import concourse.mybir as mybir
+from concourse.masks import make_identity
+
+B, L, D, R = 4, 384, 1024, 1024
+FLOPS = 2 * B * L * D * (2 * R) + 2 * B * L * L * R
+
+F32 = mybir.dt.float32
+BF16 = mybir.dt.bfloat16
+U32 = mybir.dt.uint32
+U8 = mybir.dt.uint8
+E4M3 = mybir.dt.float8_e4m3fn
+X4 = mybir.dt.float8_e4m3fn_x4
+ALU = mybir.AluOpType
+ACT = mybir.ActivationFunctionType
+AX = mybir.AxisListType
+
+P = 128
+NB = L // P
+SPLIT = ((0, 256), (256, 384))
+DEP, HEAD = 0, 1
+SLOPE = 0.1
+MANUAL = False
+
+
+def tile_biaffine_arc_scores_f5_kernel(tc, x_bytes, x_scale, w_dep, b_dep, w_head, b_head, u, v, pos, out_0, out_1):
+    nc = tc.nc
+    with ExitStack() as ctx:
+        keep = ctx.enter_context(tc.tile_pool(name="keep", bufs=1))
+        raws = ctx.enter_context(tc.tile_pool(name="raws", bufs=8))
+        wgs = ctx.enter_context(tc.tile_pool(name="wgs", bufs=4))
+        xbs = ctx.enter_context(tc.tile_pool(name="xbs", bufs=4))
+        xgs = ctx.enter_context(tc.tile_pool(name="xgs", bufs=2))
+        zs = ctx.enter_context(tc.tile_pool(name="zs", bufs=2))
+        gs = ctx.enter_context(tc.tile_pool(name="gs", bufs=2))
+        cods = ctx.enter_context(tc.tile_pool(name="cods", bufs=2))
+        soft = ctx.enter_context(tc.tile_pool(name="soft", bufs=4))
+        ps1 = ctx.enter_context(tc.psum_pool(name="ps1", bufs=5))
+        ps2 = ctx.enter_context(tc.psum_pool(name="ps2", bufs=3))
+        if MANUAL:
+            ctx.enter_context(tc.manual_schedule())
+
+        vec_raw = []
+        scl = keep.tile([P, D], F32, name="scl")
+        nc.scalar.dma_start(out=scl[:], in_=x_scale.rearrange("o k -> (o k)").partition_broadcast(P))
+        for i, vec in enumerate((b_dep, b_head, u, v)):
+            raw_v = keep.tile([P, 2, 4], BF16, name="raw_v%d" % i)
+            nc.scalar.dma_start(out=raw_v[:], in_=vec.rearrange("(g p t) -> p g t", p=P, t=4))
+            vec_raw.append(raw_v)
+        xby = {}
+
+        def x_load(s, b0, b1):
+            xbyt = keep.tile([P, b1 - b0, D], U8, name="xbyt%d%d" % (s, b0))
+            nc.sync.dma_start(out=xbyt[:], in_=x_bytes[s * L + b0 * P:s * L + b1 * P, :].rearrange("(b p) k -> p b k", p=P))
+            for b in range(b0, b1):
+                xby[s, b] = xbyt[:, b - b0, :]
+
+        w_hbm = (w_dep, w_head)
+        raw = {}
+
+        def w_load(m, g, d):
+            wr = raws.tile([P, 4, 512], BF16, name="wr", tag="wr", align_bytes=64)
+            nc.sync.dma_start(out=wr[:], in_=w_hbm[m][d * 512:(d + 1) * 512, g * 512:(g + 1) * 512].rearrange("(p j) c -> p j c", j=4))
+            raw[m, g, d] = wr
+
+        x_load(0, 0, 1)
+        w_load(DEP, 0, 0)
+        x_load(0, 1, 3)
+        w_load(DEP, 0, 1)
+        w_load(HEAD, 0, 0)
+        w_load(HEAD, 0, 1)
+        x_load(1, 0, 3)
+        w_load(DEP, 1, 0)
+        w_load(DEP, 1, 1)
+        w_load(HEAD, 1, 0)
+        w_load(HEAD, 1, 1)
+        x_load(2, 0, 3)
+        x_load(3, 0, 3)
+        pos_sb = keep.tile([P, NB, L], BF16, name="pos_sb")
+        nc.sync.dma_start(out=pos_sb[:], in_=pos.rearrange("(b p) j -> p b j", p=P))
+
+        ident_f = keep.tile([P, P], F32, name="ident_f")
+        make_identity(nc, ident_f[:])
+        ident_b = keep.tile([P, P], BF16, name="ident_b")
+        nc.gpsimd.tensor_copy(out=ident_b[:], in_=ident_f[:])
+        vecs = []
+        for i in range(4):
+            full = keep.tile([P, 2, 4], F32, name="full%d" % i)
+            nc.gpsimd.tensor_copy(out=full[:], in_=vec_raw[i][:])
+            vecs.append(full)
+        bd, bh, uu, vv = vecs
+        bd_s = keep.tile([P, 2, 4], F32, name="bd_s")
+        nc.gpsimd.tensor_scalar(out=bd_s[:], in0=bd[:], scalar1=SLOPE, scalar2=None, op0=ALU.mult)
+        warm = keep.tile([P, 1], F32, name="warm")
+        nc.vector.memset(warm[:], 0.0)
+        nc.scalar.activation(out=warm[:], in_=warm[:], func=ACT.Exp)
+
+        w_codes, w_scales = {}, {}
+
+        w_grp = {}
+
+        def w_turn(m, g, d, engines):
+            wg = wgs.tile([P, 2048], BF16, name="wg", tag="wg", align_bytes=64)
+            view = raw[m, g, d][:].rearrange("p j (m t) -> p t m j", t=4)
+            for h in range(2):
+                bank = ps2.tile([P, 1024], BF16, name="wbank", tag="aux")
+                for e in range(2):
+                    nc.tensor.matmul(out=bank[:, e * 512:(e + 1) * 512].rearrange("p (m j) -> p m j", j=4), lhsT=ident_b[:], rhs=view[:, 2 * h + e], start=True, stop=True)
+                if engines[h] == "s":
+                    nc.scalar.copy(out=wg[:, h * 1024:(h + 1) * 1024], in_=bank[:])
+                else:
+                    nc.vector.tensor_copy(out=wg[:, h * 1024:(h + 1) * 1024], in_=bank[:])
+            w_grp[m, g, d] = wg
+
+        def w_quant(m, g, d):
+            wc = keep.tile([P, 512], U32, name="wc%d%d%d" % (m, g, d), align_bytes=64)
+            ws = keep.tile([P, 512], U8, name="ws%d%d%d" % (m, g, d), align_bytes=64)
+            nc.vector.quantize_mx(out=wc[:].bitcast(X4), scales=ws[:], in_=w_grp[m, g, d][:])
+            w_codes[m, g, d], w_scales[m, g, d] = wc, ws
+
+        x_bf, x_grp, x_codes, x_scales = {}, {}, {}, {}
+
+        def x_mul(s, b):
+            xb = xbs.tile([P, D], BF16, name="xb", tag="xb", align_bytes=64)
+            nc.vector.tensor_tensor(out=xb[:], in0=xby[s, b].bitcast(E4M3), in1=scl[:], op=ALU.mult)
+            x_bf[s, b] = xb
+
+        def x_turn(s, b):
+            if b == 0:
+                x_grp[s] = xgs.tile([P, 2, L, 2], F32, name="xg", tag="xg", align_bytes=64)
+            words = x_bf[s, b][:].bitcast(F32)
+            bank = ps2.tile([P, 2, 2, P], F32, name="xbank", tag="aux")
+            for d in range(2):
+                for w in range(2):
+                    nc.tensor.transpose(bank[:, d, w, :], words[:, 256 * d + w:256 * (d + 1):2], ident_f[:])
+            nc.scalar.copy(out=x_grp[s][:, :, b * P:(b + 1) * P, :], in_=bank[:].rearrange("p d w r -> p d r w"))
+
+        def x_quant(s):
+            xc = cods.tile([P, 2 * L], U32, name="xc", tag="xc", align_bytes=64)
+            xs = cods.tile([P, 2 * L], U8, name="xs", tag="xs", align_bytes=64)
+            flat = x_grp[s][:].rearrange("p d n w -> p (d n w)").bitcast(BF16)
+            for a, e in ((0, 512), (512, 768)):
+                nc.vector.quantize_mx(out=xc[:, a:e].bitcast(X4), scales=xs[:, a:e], in_=flat[:, 4 * a:4 * e])
+            x_codes[s], x_scales[s] = xc, xs
+
+        codes = {}
+
+        def get_codes(m, s):
+            if (m, s) not in codes:
+                c = cods.tile([P, 2, L], U32, name="c%d" % m, tag="c%d" % m, align_bytes=64)
+                sc = cods.tile([P, 2, L], U8, name="s%d" % m, tag="s%d" % m, align_bytes=64)
+                codes[m, s] = (c, sc)
+            return codes[m, s]
+
+        def project(m, s, g, t):
+            bank = ps1.tile([P, L], F32, name="bank1", tag="st1")
+            for a, e in SPLIT:
+                for d in range(2):
+                    nc.tensor.matmul_mx(
+                        out=bank[:, a:e],
+                        lhsT=w_codes[m, g, d][:, t * P:(t + 1) * P].bitcast(X4),
+                        lhsT_scale=w_scales[m, g, d][:, t * P:(t + 1) * P],
+                        rhs=x_codes[s][:, d * L + a:d * L + e].bitcast(X4),
+                        rhs_scale=x_scales[s][:, d * L + a:d * L + e],
+                        start=(d == 0), stop=(d == 1))
+            return bank
+
+        z_t, q_t, grp = {}, {}, {}
+
+        def dep_s(s, g, t, bank):
+            if t == 0:
+                z_t[DEP, s, g] = zs.tile([P, 4, L], F32, name="zd", tag="zd")
+            nc.scalar.activation(out=z_t[DEP, s, g][:, t, :], in_=bank[:], func=ACT.Identity, bias=bd_s[:, g, t:t + 1], scale=SLOPE)
+
+        def dep_v(s, g, t, bank):
+            if t == 0:
+                q_t[s, g] = (zs.tile([P, 4, L], F32, name="dp", tag="dp"), zs.tile([P, 4, L], BF16, name="qp", tag="qp"))
+            dp, qp = q_t[s, g]
+            nc.vector.scalar_tensor_tensor(out=dp[:, t, :], in0=bank[:], scalar=bd[:, g, t:t + 1], in1=z_t[DEP, s, g][:, t, :], op0=ALU.add, op1=ALU.max)
+            nc.gpsimd.tensor_scalar(out=qp[:, t, :], in0=dp[:, t, :], scalar1=uu[:, g, t:t + 1], scalar2=vv[:, g, t:t + 1], op0=ALU.mult, op1=ALU.add)
+
+        def dep_i(s, g):
+            gr = gs.tile([P, L, 4], BF16, name="gq", tag="gq", align_bytes=64)
+            nc.scalar.copy(out=gr[:], in_=q_t[s, g][1][:].rearrange("p t n -> p n t"))
+            grp[DEP, s, g] = gr
+
+        def head_s(s, g, t, bank):
+            if t == 0:
+                z_t[HEAD, s, g] = zs.tile([P, 4, L], F32, name="zh", tag="zh")
+            nc.scalar.activation(out=z_t[HEAD, s, g][:, t, :], in_=bank[:], func=ACT.Identity, bias=bh[:, g, t:t + 1], scale=1.0)
+
+        def head_v(s, g):
+            gr = gs.tile([P, L, 4], BF16, name="gh", tag="gh", align_bytes=64)
+            zz = z_t[HEAD, s, g][:].rearrange("p t n -> p n t")
+            nc.vector.scalar_tensor_tensor(out=gr[:], in0=zz, scalar=SLOPE, in1=zz, op0=ALU.mult, op1=ALU.max)
+            grp[HEAD, s, g] = gr
+
+        def quant(m, s, g):
+            c, sc = get_codes(m, s)
+            flat = grp[m, s, g][:].rearrange("p n t -> p (n t)")
+            for a, e in SPLIT:
+                nc.vector.quantize_mx(out=c[:, g, a:e].bitcast(X4), scales=sc[:, g, a:e], in_=flat[:, 4 * a:4 * e])
+
+        st = {}
+
+        def score_mm(s, i):
+            (qc, qs), (hc, hs) = codes[DEP, s], codes[HEAD, s]
+            bank = ps2.tile([P, L], F32, name="sbank", tag="aux")
+            for a, e in SPLIT:
+                for g in range(2):
+                    nc.tensor.matmul_mx(
+                        out=bank[:, a:e],
+                        lhsT=qc[:, g, i * P:(i + 1) * P].bitcast(X4), lhsT_scale=qs[:, g, i * P:(i + 1) * P],
+                        rhs=hc[:, g, a:e].bitcast(X4), rhs_scale=hs[:, g, a:e],
+                        start=(g == 0), stop=(g == 1))
+            st[s, i] = bank
+
+        def score_v(s, i):
+            sc = soft.tile([P, L], F32, name="sc", tag="sc")
+            nc.vector.scalar_tensor_tensor(out=sc[:], in0=st[s, i][:], scalar=1.0 / 32.0, in1=pos_sb[:, i, :], op0=ALU.mult, op1=ALU.add)
+            nc.sync.dma_start(out=out_0[s, i * P:(i + 1) * P, :], in_=sc[:])
+            mx = soft.tile([P, 1], F32, name="mx", tag="mx")
+            nc.vector.tensor_reduce(out=mx[:], in_=sc[:], axis=AX.X, op=ALU.max, negate=True)
+            st[s, i] = (sc, mx)
+
+        def score_e(s, i):
+            sc, mx = st[s, i]
+            ex = soft.tile([P, L], F32, name="ex", tag="ex")
+            sm = soft.tile([P, 1], F32, name="sm", tag="sm")
+            nc.scalar.activation(out=ex[:], in_=sc[:], func=ACT.Exp, bias=mx[:], scale=1.0, accum_out=sm[:])
+            st[s, i] = (ex, sm)
+
+        def score_l(s, i):
+            ex, sm = st[s, i]
+            rc = soft.tile([P, 1], F32, name="rc", tag="rc")
+            nc.vector.reciprocal(out=rc[:], in_=sm[:])
+            lf = soft.tile([P, L], F32, name="lf", tag="lf")
+            eng = nc.gpsimd if s < B - 1 else nc.vector
+            eng.tensor_scalar(out=lf[:], in0=ex[:], scalar1=rc[:], scalar2=float(L), op0=ALU.mult, op1=ALU.mult)
+            nc.sync.dma_start(out=out_1[s, i * P:(i + 1) * P, :], in_=lf[:])
+
+        def dep_slot(s, g, before=(), mid=(), after=(), s_before=(), s_after=()):
+            for f in s_before:
+                f()
+            banks = [project(DEP, s, g, t) for t in range(4)]
+            for t in range(4):
+                dep_s(s, g, t, banks[t])
+            for f in s_after:
+                f()
+            for f in before:
+                f()
+            for t in range(4):
+                dep_v(s, g, t, banks[t])
+                if t < len(mid):
+                    mid[t]()
+            for f in after:
+                f()
+
+        def head_slot(s, g, s_before=(), v_before=(), s_mid=(), v_after=(), i_first=False):
+            for f in s_before:
+                f()
+            banks = [project(HEAD, s, g, t) for t in range(4)]
+            if i_first:
+                dep_i(s, g)
+            for t in range(4):
+                head_s(s, g, t, banks[t])
+            for f in s_mid:
+                f()
+            if not i_first:
+                dep_i(s, g)
+            for f in v_before:
+                f()
+            head_v(s, g)
+            for f in v_after:
+                f()
+
+        def call(f, *a):
+            return lambda: f(*a)
+
+        x_mul(0, 0)
+        w_turn(DEP, 0, 0, "ss")
+        x_turn(0, 0)
+        x_mul(0, 1)
+        x_mul(0, 2)
+        w_quant(DEP, 0, 0)
+        x_turn(0, 1)
+        x_turn(0, 2)
+        w_turn(DEP, 0, 1, "ss")
+        x_quant(0)
+        w_quant(DEP, 0, 1)
+        x_mul(1, 0)
+        for s in range(B):
+            prev, nxt = s - 1, s + 1
+            if s == 0:
+                dep_slot(s, 0, s_after=[call(w_turn, HEAD, 0, 0, "sv"), call(w_turn, HEAD, 0, 1, "sv")], after=[call(w_quant, HEAD, 0, 0), call(w_quant, HEAD, 0, 1), call(x_mul, 1, 1)])
+            else:
+                more = [call(x_mul, nxt, 1)] if nxt < B else []
+                more_s = [call(x_turn, nxt, 0)] if nxt < B else []
+                dep_slot(s, 0, mid=[call(quant, HEAD, prev, 1), call(quant, DEP, prev, 1)], after=more, s_after=more_s)
+            vb = []
+            if prev >= 0:
+                vb = [call(score_mm, prev, i) for i in range(NB)] + [call(score_v, prev, i) for i in range(NB)]
+            sm = []
+            if s == 0:
+                sm = [call(w_turn, DEP, 1, 0, "sv"), call(w_turn, DEP, 1, 1, "sv"), call(x_turn, 1, 0)]
+                vb = [call(w_quant, DEP, 1, 0), call(w_quant, DEP, 1, 1)]
+            head_slot(s, 0, v_before=vb, s_mid=sm)
+            sa = []
+            if prev >= 0:
+                sa += [call(score_e, prev, i) for i in range(NB)]
+            if nxt < B:
+                sa += [call(x_turn, nxt, 1)]
+            more = [call(x_mul, nxt, 2)] if nxt < B else []
+            if s == 0:
+                sa += [call(w_turn, HEAD, 1, 0, "sv"), call(w_turn, HEAD, 1, 1, "sv")]
+                more += [call(w_quant, HEAD, 1, 0), call(w_quant, HEAD, 1, 1)]
+            dep_slot(s, 1, mid=[call(quant, HEAD, s, 0), call(quant, DEP, s, 0)], after=more, s_after=sa)
+            sb, vb = [], []
+            if nxt < B:
+                sb = [call(x_turn, nxt, 2)]
+                vb = [call(x_quant, nxt)]
+            if nxt + 1 < B:
+                vb = [call(x_mul, nxt + 1, 0)] + vb
+            if prev >= 0:
+                vb += [call(score_l, prev, i) for i in range(NB)]
+            if nxt == B:
+                vb += [call(quant, DEP, s, 1)]
+            head_slot(s, 1, s_before=sb, v_before=vb, i_first=(nxt == B))
+        s = B - 1
+        quant(HEAD, s, 1)
+        for i in range(NB):
+            score_mm(s, i)
+        for i in range(NB):
+            score_v(s, i)
+            score_e(s, i)
+        for i in range(NB):
+            score_l(s, i)

@@ -22,6 +22,7 @@ SPLIT = ((0, 256), (256, 384))
 DEP, HEAD = 0, 1
 SLOPE = 0.1
 MANUAL = False
+ON_V = {(HEAD, 3, 1)}
 
 
 def tile_biaffine_arc_scores_f5_kernel(tc, x_bytes, x_scale, w_dep, b_dep, w_head, b_head, u, v, pos, out_0, out_1):
@@ -32,8 +33,9 @@ def tile_biaffine_arc_scores_f5_kernel(tc, x_bytes, x_scale, w_dep, b_dep, w_hea
         wgs = ctx.enter_context(tc.tile_pool(name="wgs", bufs=4))
         xbs = ctx.enter_context(tc.tile_pool(name="xbs", bufs=4))
         xgs = ctx.enter_context(tc.tile_pool(name="xgs", bufs=2))
-        zs = ctx.enter_context(tc.tile_pool(name="zs", bufs=2))
-        gs = ctx.enter_context(tc.tile_pool(name="gs", bufs=2))
+        zs = ctx.enter_context(tc.tile_pool(name="zs", bufs=3))
+        ks = ctx.enter_context(tc.tile_pool(name="ks", bufs=2))
+        gs = ctx.enter_context(tc.tile_pool(name="gs", bufs=3))
         cods = ctx.enter_context(tc.tile_pool(name="cods", bufs=2))
         soft = ctx.enter_context(tc.tile_pool(name="soft", bufs=4))
         ps1 = ctx.enter_context(tc.psum_pool(name="ps1", bufs=5))
@@ -168,33 +170,32 @@ def tile_biaffine_arc_scores_f5_kernel(tc, x_bytes, x_scale, w_dep, b_dep, w_hea
 
         z_t, q_t, grp = {}, {}, {}
 
-        def dep_s(s, g, t, bank):
+        def shift(m, s, g, t, bank):
             if t == 0:
-                z_t[DEP, s, g] = zs.tile([P, 4, L], F32, name="zd", tag="zd")
-            nc.scalar.activation(out=z_t[DEP, s, g][:, t, :], in_=bank[:], func=ACT.Identity, bias=bd_s[:, g, t:t + 1], scale=SLOPE)
+                z_t[m, s, g] = zs.tile([P, 4, L], F32, name="z", tag="z")
+            nc.scalar.activation(out=z_t[m, s, g][:, t, :], in_=bank[:], func=ACT.Identity, bias=(bd, bh)[m][:, g, t:t + 1], scale=1.0)
 
-        def dep_v(s, g, t, bank):
-            if t == 0:
-                q_t[s, g] = (zs.tile([P, 4, L], F32, name="dp", tag="dp"), zs.tile([P, 4, L], BF16, name="qp", tag="qp"))
-            dp, qp = q_t[s, g]
-            nc.vector.scalar_tensor_tensor(out=dp[:, t, :], in0=bank[:], scalar=bd[:, g, t:t + 1], in1=z_t[DEP, s, g][:, t, :], op0=ALU.add, op1=ALU.max)
-            nc.gpsimd.tensor_scalar(out=qp[:, t, :], in0=dp[:, t, :], scalar1=uu[:, g, t:t + 1], scalar2=vv[:, g, t:t + 1], op0=ALU.mult, op1=ALU.add)
+        def kink(m, s, g):
+            z = z_t[m, s, g]
+            k = ks.tile([P, 4, L], F32 if m == DEP else BF16, name="k%d" % m, tag="k%d" % m)
+            nc.vector.scalar_tensor_tensor(out=k[:], in0=z[:], scalar=SLOPE, in1=z[:], op0=ALU.mult, op1=ALU.max)
+            if m == HEAD:
+                q_t[m, s, g] = k
+            else:
+                q = ks.tile([P, 4, L], BF16, name="q", tag="q")
+                for t in range(4):
+                    nc.vector.tensor_scalar(out=q[:, t, :], in0=k[:, t, :], scalar1=uu[:, g, t:t + 1], scalar2=vv[:, g, t:t + 1], op0=ALU.mult, op1=ALU.add)
+                q_t[m, s, g] = q
 
-        def dep_i(s, g):
-            gr = gs.tile([P, L, 4], BF16, name="gq", tag="gq", align_bytes=64)
-            nc.scalar.copy(out=gr[:], in_=q_t[s, g][1][:].rearrange("p t n -> p n t"))
-            grp[DEP, s, g] = gr
-
-        def head_s(s, g, t, bank):
-            if t == 0:
-                z_t[HEAD, s, g] = zs.tile([P, 4, L], F32, name="zh", tag="zh")
-            nc.scalar.activation(out=z_t[HEAD, s, g][:, t, :], in_=bank[:], func=ACT.Identity, bias=bh[:, g, t:t + 1], scale=1.0)
-
-        def head_v(s, g):
-            gr = gs.tile([P, L, 4], BF16, name="gh", tag="gh", align_bytes=64)
-            zz = z_t[HEAD, s, g][:].rearrange("p t n -> p n t")
-            nc.vector.scalar_tensor_tensor(out=gr[:], in0=zz, scalar=SLOPE, in1=zz, op0=ALU.mult, op1=ALU.max)
-            grp[HEAD, s, g] = gr
+        def inter(m, s, g):
+            gr = gs.tile([P, L, 4], BF16, name="gr", tag="gr", align_bytes=64)
+            dst = gr[:].rearrange("p (c i) t -> p c t i", i=4)
+            sr = q_t[m, s, g][:].rearrange("p t (c i) -> p c t i", i=4)
+            if (m, s, g) in ON_V:
+                nc.vector.tensor_copy(out=dst, in_=sr)
+            else:
+                nc.scalar.copy(out=dst, in_=sr)
+            grp[m, s, g] = gr
 
         def quant(m, s, g):
             c, sc = get_codes(m, s)
@@ -236,47 +237,16 @@ def tile_biaffine_arc_scores_f5_kernel(tc, x_bytes, x_scale, w_dep, b_dep, w_hea
             rc = soft.tile([P, 1], F32, name="rc", tag="rc")
             nc.vector.reciprocal(out=rc[:], in_=sm[:])
             lf = soft.tile([P, L], F32, name="lf", tag="lf")
-            eng = nc.gpsimd if s < B - 1 else nc.vector
+            eng = nc.vector
             eng.tensor_scalar(out=lf[:], in0=ex[:], scalar1=rc[:], scalar2=float(L), op0=ALU.mult, op1=ALU.mult)
             nc.sync.dma_start(out=out_1[s, i * P:(i + 1) * P, :], in_=lf[:])
 
-        def dep_slot(s, g, before=(), mid=(), after=(), s_before=(), s_after=()):
-            for f in s_before:
-                f()
-            banks = [project(DEP, s, g, t) for t in range(4)]
-            for t in range(4):
-                dep_s(s, g, t, banks[t])
-            for f in s_after:
-                f()
-            for f in before:
-                f()
-            for t in range(4):
-                dep_v(s, g, t, banks[t])
-                if t < len(mid):
-                    mid[t]()
-            for f in after:
-                f()
-
-        def head_slot(s, g, s_before=(), v_before=(), s_mid=(), v_after=(), i_first=False):
-            for f in s_before:
-                f()
-            banks = [project(HEAD, s, g, t) for t in range(4)]
-            if i_first:
-                dep_i(s, g)
-            for t in range(4):
-                head_s(s, g, t, banks[t])
-            for f in s_mid:
-                f()
-            if not i_first:
-                dep_i(s, g)
-            for f in v_before:
-                f()
-            head_v(s, g)
-            for f in v_after:
-                f()
-
         def call(f, *a):
             return lambda: f(*a)
+
+        def proj(m, s, g):
+            for t in range(4):
+                shift(m, s, g, t, project(m, s, g, t))
 
         x_mul(0, 0)
         w_turn(DEP, 0, 0, "ss")
@@ -290,45 +260,49 @@ def tile_biaffine_arc_scores_f5_kernel(tc, x_bytes, x_scale, w_dep, b_dep, w_hea
         x_quant(0)
         w_quant(DEP, 0, 1)
         x_mul(1, 0)
-        for s in range(B):
-            prev, nxt = s - 1, s + 1
-            if s == 0:
-                dep_slot(s, 0, s_after=[call(w_turn, HEAD, 0, 0, "sv"), call(w_turn, HEAD, 0, 1, "sv")], after=[call(w_quant, HEAD, 0, 0), call(w_quant, HEAD, 0, 1), call(x_mul, 1, 1)])
-            else:
-                more = [call(x_mul, nxt, 1)] if nxt < B else []
-                more_s = [call(x_turn, nxt, 0)] if nxt < B else []
-                dep_slot(s, 0, mid=[call(quant, HEAD, prev, 1), call(quant, DEP, prev, 1)], after=more, s_after=more_s)
-            vb = []
-            if prev >= 0:
-                vb = [call(score_mm, prev, i) for i in range(NB)] + [call(score_v, prev, i) for i in range(NB)]
-            sm = []
-            if s == 0:
-                sm = [call(w_turn, DEP, 1, 0, "sv"), call(w_turn, DEP, 1, 1, "sv"), call(x_turn, 1, 0)]
-                vb = [call(w_quant, DEP, 1, 0), call(w_quant, DEP, 1, 1)]
-            head_slot(s, 0, v_before=vb, s_mid=sm)
-            sa = []
-            if prev >= 0:
-                sa += [call(score_e, prev, i) for i in range(NB)]
+        proj(DEP, 0, 0)
+        tasks = [(s, g, m) for s in range(B) for g in range(2) for m in (DEP, HEAD)]
+        for n, (s, g, m) in enumerate(tasks):
+            if n + 1 < len(tasks):
+                s1, g1, m1 = tasks[n + 1]
+                if s1 == 0:
+                    for d in range(2):
+                        w_turn(m1, g1, d, "ss")
+                        w_quant(m1, g1, d)
+                proj(m1, s1, g1)
+            kink(m, s, g)
+            if n >= 1:
+                s0, g0, m0 = tasks[n - 1]
+                quant(m0, s0, g0)
+            inter(m, s, g)
+            k = n % 4
+            nxt = s + 1
+            if k == 0 and s >= 1:
+                for i in range(NB):
+                    score_mm(s - 1, i)
+            if k == 1 and s >= 1:
+                for i in range(NB):
+                    score_v(s - 1, i)
+                for i in range(NB):
+                    score_e(s - 1, i)
+            if k == 2 and s >= 1:
+                for i in range(NB):
+                    score_l(s - 1, i)
             if nxt < B:
-                sa += [call(x_turn, nxt, 1)]
-            more = [call(x_mul, nxt, 2)] if nxt < B else []
-            if s == 0:
-                sa += [call(w_turn, HEAD, 1, 0, "sv"), call(w_turn, HEAD, 1, 1, "sv")]
-                more += [call(w_quant, HEAD, 1, 0), call(w_quant, HEAD, 1, 1)]
-            dep_slot(s, 1, mid=[call(quant, HEAD, s, 0), call(quant, DEP, s, 0)], after=more, s_after=sa)
-            sb, vb = [], []
-            if nxt < B:
-                sb = [call(x_turn, nxt, 2)]
-                vb = [call(x_quant, nxt)]
-            if nxt + 1 < B:
-                vb = [call(x_mul, nxt + 1, 0)] + vb
-            if prev >= 0:
-                vb += [call(score_l, prev, i) for i in range(NB)]
-            if nxt == B:
-                vb += [call(quant, DEP, s, 1)]
-            head_slot(s, 1, s_before=sb, v_before=vb, i_first=(nxt == B))
+                if k == 0:
+                    x_turn(nxt, 0)
+                    x_mul(nxt, 1)
+                if k == 1:
+                    x_turn(nxt, 1)
+                    x_mul(nxt, 2)
+                if k == 2:
+                    x_turn(nxt, 2)
+                    x_quant(nxt)
+                    if nxt + 1 < B:
+                        x_mul(nxt + 1, 0)
+        s0, g0, m0 = tasks[-1]
+        quant(m0, s0, g0)
         s = B - 1
-        quant(HEAD, s, 1)
         for i in range(NB):
             score_mm(s, i)
         for i in range(NB):

@@ -43,13 +43,14 @@ def tile_biaffine_arc_scores_f5_kernel(tc, x_bytes, x_scale, w_dep, b_dep, w_hea
         if MANUAL:
             ctx.enter_context(tc.manual_schedule())
 
-        vec_raw = []
         scl = keep.tile([P, D], F32, name="scl")
         nc.scalar.dma_start(out=scl[:], in_=x_scale.rearrange("o k -> (o k)").partition_broadcast(P))
+        vrow = keep.tile([P, P], BF16, name="vrow")
+        nc.gpsimd.memset(vrow[:], 0.0)
         for i, vec in enumerate((b_dep, b_head, u, v)):
-            raw_v = keep.tile([P, 2, 4], BF16, name="raw_v%d" % i)
-            nc.scalar.dma_start(out=raw_v[:], in_=vec.rearrange("(g p t) -> p g t", p=P, t=4))
-            vec_raw.append(raw_v)
+            for g in range(2):
+                r = 8 * i + 4 * g
+                nc.gpsimd.dma_start(out=vrow[r:r + 4, :].rearrange("t (b i) -> t b i", i=8), in_=vec[g * 512:(g + 1) * 512].rearrange("(b t i) -> t b i", t=4, i=8))
         xby = {}
 
         def x_load(s, b0, b1):
@@ -86,17 +87,16 @@ def tile_biaffine_arc_scores_f5_kernel(tc, x_bytes, x_scale, w_dep, b_dep, w_hea
         make_identity(nc, ident_f[:])
         ident_b = keep.tile([P, P], BF16, name="ident_b")
         nc.gpsimd.tensor_copy(out=ident_b[:], in_=ident_f[:])
-        vecs = []
-        for i in range(4):
-            full = keep.tile([P, 2, 4], F32, name="full%d" % i)
-            nc.gpsimd.tensor_copy(out=full[:], in_=vec_raw[i][:])
-            vecs.append(full)
-        bd, bh, uu, vv = vecs
-        bd_s = keep.tile([P, 2, 4], F32, name="bd_s")
-        nc.gpsimd.tensor_scalar(out=bd_s[:], in0=bd[:], scalar1=SLOPE, scalar2=None, op0=ALU.mult)
+        vcol = keep.tile([P, 4, 2, 4], F32, name="vcol")
+        bd, bh, uu, vv = (vcol[:, i] for i in range(4))
         warm = keep.tile([P, 1], F32, name="warm")
         nc.vector.memset(warm[:], 0.0)
         nc.scalar.activation(out=warm[:], in_=warm[:], func=ACT.Exp)
+
+        def load_vectors():
+            bank = ps2.tile([P, P], BF16, name="vbank", tag="aux")
+            nc.tensor.transpose(bank[:], vrow[:], ident_b[:])
+            nc.vector.tensor_copy(out=vcol[:].rearrange("p i g t -> p (i g t)"), in_=bank[:, 0:32])
 
         w_codes, w_scales = {}, {}
 
@@ -104,15 +104,13 @@ def tile_biaffine_arc_scores_f5_kernel(tc, x_bytes, x_scale, w_dep, b_dep, w_hea
 
         def w_turn(m, g, d, engines):
             wg = wgs.tile([P, 2048], BF16, name="wg", tag="wg", align_bytes=64)
-            view = raw[m, g, d][:].rearrange("p j (m t) -> p t m j", t=4)
-            for h in range(2):
-                bank = ps2.tile([P, 1024], BF16, name="wbank", tag="aux")
-                for e in range(2):
-                    nc.tensor.matmul(out=bank[:, e * 512:(e + 1) * 512].rearrange("p (m j) -> p m j", j=4), lhsT=ident_b[:], rhs=view[:, 2 * h + e], start=True, stop=True)
-                if engines[h] == "s":
-                    nc.scalar.copy(out=wg[:, h * 1024:(h + 1) * 1024], in_=bank[:])
+            view = raw[m, g, d][:].rearrange("p j (b t i) -> p t b i j", t=4, i=8)
+            out = wg[:].rearrange("p (t b i j) -> p t b i j", t=4, i=8, j=4)
+            for t in range(4):
+                if engines[t] == "s":
+                    nc.scalar.copy(out=out[:, t], in_=view[:, t])
                 else:
-                    nc.vector.tensor_copy(out=wg[:, h * 1024:(h + 1) * 1024], in_=bank[:])
+                    nc.vector.tensor_copy(out=out[:, t], in_=view[:, t])
             w_grp[m, g, d] = wg
 
         def w_quant(m, g, d):
@@ -189,8 +187,8 @@ def tile_biaffine_arc_scores_f5_kernel(tc, x_bytes, x_scale, w_dep, b_dep, w_hea
 
         def inter(m, s, g):
             gr = gs.tile([P, L, 4], BF16, name="gr", tag="gr", align_bytes=64)
-            dst = gr[:].rearrange("p (c i) t -> p c t i", i=4)
-            sr = q_t[m, s, g][:].rearrange("p t (c i) -> p c t i", i=4)
+            dst = gr[:]
+            sr = q_t[m, s, g][:].rearrange("p t n -> p n t")
             if (m, s, g) in ON_V:
                 nc.vector.tensor_copy(out=dst, in_=sr)
             else:
@@ -249,17 +247,18 @@ def tile_biaffine_arc_scores_f5_kernel(tc, x_bytes, x_scale, w_dep, b_dep, w_hea
                 shift(m, s, g, t, project(m, s, g, t))
 
         x_mul(0, 0)
-        w_turn(DEP, 0, 0, "ss")
+        w_turn(DEP, 0, 0, "vvss")
         x_turn(0, 0)
         x_mul(0, 1)
         x_mul(0, 2)
         w_quant(DEP, 0, 0)
         x_turn(0, 1)
         x_turn(0, 2)
-        w_turn(DEP, 0, 1, "ss")
+        w_turn(DEP, 0, 1, "vvss")
         x_quant(0)
         w_quant(DEP, 0, 1)
         x_mul(1, 0)
+        load_vectors()
         proj(DEP, 0, 0)
         tasks = [(s, g, m) for s in range(B) for g in range(2) for m in (DEP, HEAD)]
         for n, (s, g, m) in enumerate(tasks):
@@ -267,7 +266,7 @@ def tile_biaffine_arc_scores_f5_kernel(tc, x_bytes, x_scale, w_dep, b_dep, w_hea
                 s1, g1, m1 = tasks[n + 1]
                 if s1 == 0:
                     for d in range(2):
-                        w_turn(m1, g1, d, "ss")
+                        w_turn(m1, g1, d, "vvss")
                         w_quant(m1, g1, d)
                 proj(m1, s1, g1)
             kink(m, s, g)

@@ -1,4 +1,5 @@
 from contextlib import ExitStack
+from functools import partial
 
 import concourse.mybir as mybir
 from concourse.masks import make_identity
@@ -21,8 +22,25 @@ NB = L // P
 SPLIT = ((0, 256), (256, 384))
 DEP, HEAD = 0, 1
 SLOPE = 0.1
-MANUAL = False
-ON_V = {(HEAD, 3, 1)}
+MANUAL = True
+ON_V = set()
+ON_G = set()
+VM = set()
+WE = "vvss"
+AFF = "gggg"
+TPL = {
+    "g0": "H0 Z0 H1 H2 Z1 H3 D0 X1 Z2 D2 S0 D1 Z3 S1 lg D3 X2 S2 ex T0 rc K0 T1 L T2 K1 st S3 K3 rc I K2 ex sc qh qd lf sc".split(),
+    "g1": "H2 rc H3 X0 H0 lf xq Z0 H1 ex Z3 Z1 rc Z2 lg D0 ex L S0 D1 K0 D2 S1 D3 S2 S3 K1 K2 K3 I sc qh qd".split(),
+    "first": "wd0c H2 H3 H1 X1 wd0q H0 wd1c Z0 Z1 Z2 Z3 wh0c wh1c wd1q D1 D0 L D3 S0 S3 S1 D2 T0 X2 S2 I K0 wh0q T2 T1 K1 wh1q K2 K3 qh qd".split(),
+    "last": "H0 Z0 H1 rc Z1 H3 I H2 Z3 sc Z2 qd ex ex lf L qh rc lf".split(),
+    "pro": "cD0s m00b m00a cD0v t0 m01 m02 cD1s t1 qD0 cH0s cD1v t2 cH1v lv qD1 cH1s xq m10 D0 qH1 D1 S0 K0 S1 D2 D3 cH0v S2 K2 qH0 S3 K1 K3".split(),
+    "tail": "mm0 mm1 rc sc0 mm2 sc1 ex mx0 mx1 ex0 sc2 rc ex1 lfv mx2 rc0 lfv rc1 sc ex2 rc ex lfv lf0v lf1v rc2 lfv lfv rc rc lf2v".split(),
+}
+WK = (0, 2)
+WP = {"D0":2,"D1":2,"H0":3,"H1":1}
+PF = True
+HS = True
+LG = "v"
 
 
 def tile_biaffine_arc_scores_f5_kernel(tc, x_bytes, x_scale, w_dep, b_dep, w_head, b_head, u, v, pos, out_0, out_1):
@@ -37,20 +55,21 @@ def tile_biaffine_arc_scores_f5_kernel(tc, x_bytes, x_scale, w_dep, b_dep, w_hea
         ks = ctx.enter_context(tc.tile_pool(name="ks", bufs=2))
         gs = ctx.enter_context(tc.tile_pool(name="gs", bufs=3))
         cods = ctx.enter_context(tc.tile_pool(name="cods", bufs=2))
-        soft = ctx.enter_context(tc.tile_pool(name="soft", bufs=4))
+        soft = ctx.enter_context(tc.tile_pool(name="soft", bufs=6))
         ps1 = ctx.enter_context(tc.psum_pool(name="ps1", bufs=5))
         ps2 = ctx.enter_context(tc.psum_pool(name="ps2", bufs=3))
         if MANUAL:
             ctx.enter_context(tc.manual_schedule())
 
-        scl = keep.tile([P, D], F32, name="scl")
-        nc.scalar.dma_start(out=scl[:], in_=x_scale.rearrange("o k -> (o k)").partition_broadcast(P))
+        ident_f = keep.tile([P, P], F32, name="ident_f")
+        make_identity(nc, ident_f[:])
+        ident_b = keep.tile([P, P], BF16, name="ident_b")
+        nc.gpsimd.tensor_copy(out=ident_b[:], in_=ident_f[:])
         vrow = keep.tile([P, P], BF16, name="vrow")
-        nc.gpsimd.memset(vrow[:], 0.0)
-        for i, vec in enumerate((b_dep, b_head, u, v)):
-            for g in range(2):
-                r = 8 * i + 4 * g
-                nc.gpsimd.dma_start(out=vrow[r:r + 4, :].rearrange("t (b i) -> t b i", i=8), in_=vec[g * 512:(g + 1) * 512].rearrange("(b t i) -> t b i", t=4, i=8))
+        nc.vector.memset(vrow[:], 0.0)
+        scl = keep.tile([P, D], F32, name="scl")
+        for h in range(2):
+            nc.scalar.dma_start(out=scl[:, h * 512:(h + 1) * 512], in_=x_scale[:, h * 512:(h + 1) * 512].rearrange("o k -> (o k)").partition_broadcast(P))
         xby = {}
 
         def x_load(s, b0, b1):
@@ -59,6 +78,10 @@ def tile_biaffine_arc_scores_f5_kernel(tc, x_bytes, x_scale, w_dep, b_dep, w_hea
             for b in range(b0, b1):
                 xby[s, b] = xbyt[:, b - b0, :]
 
+        for i, vec in enumerate((b_dep, b_head, u, v)):
+            for g in range(2):
+                r = 8 * i + 4 * g
+                nc.scalar.dma_start(out=vrow[r:r + 4, :].rearrange("t (b i) -> t b i", i=8), in_=vec[g * 512:(g + 1) * 512].rearrange("(b t i) -> t b i", t=4, i=8))
         w_hbm = (w_dep, w_head)
         raw = {}
 
@@ -83,12 +106,9 @@ def tile_biaffine_arc_scores_f5_kernel(tc, x_bytes, x_scale, w_dep, b_dep, w_hea
         pos_sb = keep.tile([P, NB, L], BF16, name="pos_sb")
         nc.sync.dma_start(out=pos_sb[:], in_=pos.rearrange("(b p) j -> p b j", p=P))
 
-        ident_f = keep.tile([P, P], F32, name="ident_f")
-        make_identity(nc, ident_f[:])
-        ident_b = keep.tile([P, P], BF16, name="ident_b")
-        nc.gpsimd.tensor_copy(out=ident_b[:], in_=ident_f[:])
         vcol = keep.tile([P, 4, 2, 4], F32, name="vcol")
         bd, bh, uu, vv = (vcol[:, i] for i in range(4))
+        bd_s = keep.tile([P, 2, 4], F32, name="bd_s")
         warm = keep.tile([P, 1], F32, name="warm")
         nc.vector.memset(warm[:], 0.0)
         nc.scalar.activation(out=warm[:], in_=warm[:], func=ACT.Exp)
@@ -97,21 +117,22 @@ def tile_biaffine_arc_scores_f5_kernel(tc, x_bytes, x_scale, w_dep, b_dep, w_hea
             bank = ps2.tile([P, P], BF16, name="vbank", tag="aux")
             nc.tensor.transpose(bank[:], vrow[:], ident_b[:])
             nc.vector.tensor_copy(out=vcol[:].rearrange("p i g t -> p (i g t)"), in_=bank[:, 0:32])
+            nc.gpsimd.tensor_scalar(out=bd_s[:], in0=bd, scalar1=SLOPE, scalar2=None, op0=ALU.mult)
 
         w_codes, w_scales = {}, {}
 
         w_grp = {}
 
-        def w_turn(m, g, d, engines):
-            wg = wgs.tile([P, 2048], BF16, name="wg", tag="wg", align_bytes=64)
+        def w_copy(m, g, d, slots, engine):
+            if (m, g, d) not in w_grp:
+                w_grp[m, g, d] = wgs.tile([P, 2048], BF16, name="wg", tag="wg", align_bytes=64)
             view = raw[m, g, d][:].rearrange("p j (b t i) -> p t b i j", t=4, i=8)
-            out = wg[:].rearrange("p (t b i j) -> p t b i j", t=4, i=8, j=4)
-            for t in range(4):
-                if engines[t] == "s":
+            out = w_grp[m, g, d][:].rearrange("p (t b i j) -> p t b i j", t=4, i=8, j=4)
+            for t in slots:
+                if engine == "s":
                     nc.scalar.copy(out=out[:, t], in_=view[:, t])
                 else:
                     nc.vector.tensor_copy(out=out[:, t], in_=view[:, t])
-            w_grp[m, g, d] = wg
 
         def w_quant(m, g, d):
             wc = keep.tile([P, 512], U32, name="wc%d%d%d" % (m, g, d), align_bytes=64)
@@ -121,10 +142,11 @@ def tile_biaffine_arc_scores_f5_kernel(tc, x_bytes, x_scale, w_dep, b_dep, w_hea
 
         x_bf, x_grp, x_codes, x_scales = {}, {}, {}, {}
 
-        def x_mul(s, b):
-            xb = xbs.tile([P, D], BF16, name="xb", tag="xb", align_bytes=64)
-            nc.vector.tensor_tensor(out=xb[:], in0=xby[s, b].bitcast(E4M3), in1=scl[:], op=ALU.mult)
-            x_bf[s, b] = xb
+        def x_mul(s, b, half=""):
+            if (s, b) not in x_bf:
+                x_bf[s, b] = xbs.tile([P, D], BF16, name="xb", tag="xb", align_bytes=64)
+            for h in ((0, 1024),) if half == "" else (((0, 512),) if half == "a" else ((512, 1024),)):
+                nc.vector.tensor_tensor(out=x_bf[s, b][:, h[0]:h[1]], in0=xby[s, b][:, h[0]:h[1]].bitcast(E4M3), in1=scl[:, h[0]:h[1]], op=ALU.mult)
 
         def x_turn(s, b):
             if b == 0:
@@ -168,32 +190,39 @@ def tile_biaffine_arc_scores_f5_kernel(tc, x_bytes, x_scale, w_dep, b_dep, w_hea
 
         z_t, q_t, grp = {}, {}, {}
 
-        def shift(m, s, g, t, bank):
+        banks = {}
+
+        def mm(m, s, g):
+            for t in range(4):
+                banks[m, s, g, t] = project(m, s, g, t)
+
+        def dep_s(s, g, t):
             if t == 0:
-                z_t[m, s, g] = zs.tile([P, 4, L], F32, name="z", tag="z")
-            nc.scalar.activation(out=z_t[m, s, g][:, t, :], in_=bank[:], func=ACT.Identity, bias=(bd, bh)[m][:, g, t:t + 1], scale=1.0)
+                z_t[DEP, s, g] = zs.tile([P, 4, L], F32, name="zd", tag="zd")
+            nc.scalar.activation(out=z_t[DEP, s, g][:, t, :], in_=banks[DEP, s, g, t][:], func=ACT.Identity, bias=bd_s[:, g, t:t + 1], scale=SLOPE)
 
-        def kink(m, s, g):
-            z = z_t[m, s, g]
-            k = ks.tile([P, 4, L], F32 if m == DEP else BF16, name="k%d" % m, tag="k%d" % m)
-            nc.vector.scalar_tensor_tensor(out=k[:], in0=z[:], scalar=SLOPE, in1=z[:], op0=ALU.mult, op1=ALU.max)
-            if m == HEAD:
-                q_t[m, s, g] = k
-            else:
-                q = ks.tile([P, 4, L], BF16, name="q", tag="q")
-                for t in range(4):
-                    nc.vector.tensor_scalar(out=q[:, t, :], in0=k[:, t, :], scalar1=uu[:, g, t:t + 1], scalar2=vv[:, g, t:t + 1], op0=ALU.mult, op1=ALU.add)
-                q_t[m, s, g] = q
+        def dep_v(s, g, t):
+            if t == 0:
+                q_t[s, g] = (ks.tile([P, 4, L], F32, name="dp", tag="dp"), ks.tile([P, 4, L], BF16, name="qp", tag="qp"))
+            dp, qp = q_t[s, g]
+            nc.vector.scalar_tensor_tensor(out=dp[:, t, :], in0=banks[DEP, s, g, t][:], scalar=bd[:, g, t:t + 1], in1=z_t[DEP, s, g][:, t, :], op0=ALU.add, op1=ALU.max)
+            nc.gpsimd.tensor_scalar(out=qp[:, t, :], in0=dp[:, t, :], scalar1=uu[:, g, t:t + 1], scalar2=vv[:, g, t:t + 1], op0=ALU.mult, op1=ALU.add)
 
-        def inter(m, s, g):
-            gr = gs.tile([P, L, 4], BF16, name="gr", tag="gr", align_bytes=64)
-            dst = gr[:]
-            sr = q_t[m, s, g][:].rearrange("p t n -> p n t")
-            if (m, s, g) in ON_V:
-                nc.vector.tensor_copy(out=dst, in_=sr)
-            else:
-                nc.scalar.copy(out=dst, in_=sr)
-            grp[m, s, g] = gr
+        def dep_i(s, g):
+            gr = gs.tile([P, L, 4], BF16, name="gq", tag="gq", align_bytes=64)
+            nc.scalar.copy(out=gr[:], in_=q_t[s, g][1][:].rearrange("p t n -> p n t"))
+            grp[DEP, s, g] = gr
+
+        def head_s(s, g, t):
+            if t == 0:
+                z_t[HEAD, s, g] = zs.tile([P, 4, L], F32, name="zh", tag="zh")
+            nc.scalar.activation(out=z_t[HEAD, s, g][:, t, :], in_=banks[HEAD, s, g, t][:], func=ACT.Identity, bias=bh[:, g, t:t + 1], scale=1.0)
+
+        def head_v(s, g):
+            gr = gs.tile([P, L, 4], BF16, name="gh", tag="gh", align_bytes=64)
+            zz = z_t[HEAD, s, g][:].rearrange("p t n -> p n t")
+            nc.vector.scalar_tensor_tensor(out=gr[:], in0=zz, scalar=SLOPE, in1=zz, op0=ALU.mult, op1=ALU.max)
+            grp[HEAD, s, g] = gr
 
         def quant(m, s, g):
             c, sc = get_codes(m, s)
@@ -201,7 +230,7 @@ def tile_biaffine_arc_scores_f5_kernel(tc, x_bytes, x_scale, w_dep, b_dep, w_hea
             for a, e in SPLIT:
                 nc.vector.quantize_mx(out=c[:, g, a:e].bitcast(X4), scales=sc[:, g, a:e], in_=flat[:, 4 * a:4 * e])
 
-        st = {}
+        sbank, s_sc, s_mx, s_ex, s_sm, s_rc = {}, {}, {}, {}, {}, {}
 
         def score_mm(s, i):
             (qc, qs), (hc, hs) = codes[DEP, s], codes[HEAD, s]
@@ -213,99 +242,180 @@ def tile_biaffine_arc_scores_f5_kernel(tc, x_bytes, x_scale, w_dep, b_dep, w_hea
                         lhsT=qc[:, g, i * P:(i + 1) * P].bitcast(X4), lhsT_scale=qs[:, g, i * P:(i + 1) * P],
                         rhs=hc[:, g, a:e].bitcast(X4), rhs_scale=hs[:, g, a:e],
                         start=(g == 0), stop=(g == 1))
-            st[s, i] = bank
+            sbank[s, i] = bank
 
         def score_v(s, i):
             sc = soft.tile([P, L], F32, name="sc", tag="sc")
-            nc.vector.scalar_tensor_tensor(out=sc[:], in0=st[s, i][:], scalar=1.0 / 32.0, in1=pos_sb[:, i, :], op0=ALU.mult, op1=ALU.add)
+            nc.vector.scalar_tensor_tensor(out=sc[:], in0=sbank[s, i][:], scalar=1.0 / 32.0, in1=pos_sb[:, i, :], op0=ALU.mult, op1=ALU.add)
             nc.sync.dma_start(out=out_0[s, i * P:(i + 1) * P, :], in_=sc[:])
+            s_sc[s, i] = sc
+
+        def score_m(s, i):
             mx = soft.tile([P, 1], F32, name="mx", tag="mx")
-            nc.vector.tensor_reduce(out=mx[:], in_=sc[:], axis=AX.X, op=ALU.max, negate=True)
-            st[s, i] = (sc, mx)
+            nc.vector.tensor_reduce(out=mx[:], in_=s_sc[s, i][:], axis=AX.X, op=ALU.max, negate=True)
+            s_mx[s, i] = mx
 
         def score_e(s, i):
-            sc, mx = st[s, i]
+            sc, mx = s_sc[s, i], s_mx[s, i]
             ex = soft.tile([P, L], F32, name="ex", tag="ex")
             sm = soft.tile([P, 1], F32, name="sm", tag="sm")
             nc.scalar.activation(out=ex[:], in_=sc[:], func=ACT.Exp, bias=mx[:], scale=1.0, accum_out=sm[:])
-            st[s, i] = (ex, sm)
+            nc.gpsimd.tensor_scalar(out=sm[:], in0=sm[:], scalar1=1.0 / L, scalar2=None, op0=ALU.mult)
+            s_ex[s, i], s_sm[s, i] = ex, sm
 
-        def score_l(s, i):
-            ex, sm = st[s, i]
+        def score_r(s, i):
+            sm = s_sm[s, i]
             rc = soft.tile([P, 1], F32, name="rc", tag="rc")
             nc.vector.reciprocal(out=rc[:], in_=sm[:])
+            s_rc[s, i] = rc
+
+        def score_l(s, i, engine):
+            ex, rc = s_ex[s, i], s_rc[s, i]
             lf = soft.tile([P, L], F32, name="lf", tag="lf")
-            eng = nc.vector
-            eng.tensor_scalar(out=lf[:], in0=ex[:], scalar1=rc[:], scalar2=float(L), op0=ALU.mult, op1=ALU.mult)
+            if engine == "s":
+                nc.scalar.activation(out=lf[:], in_=ex[:], func=ACT.Copy, scale=rc[:])
+            elif engine == "g":
+                nc.gpsimd.tensor_scalar(out=lf[:], in0=ex[:], scalar1=rc[:], scalar2=1.0, op0=ALU.mult, op1=ALU.mult)
+            else:
+                nc.vector.tensor_scalar(out=lf[:], in0=ex[:], scalar1=rc[:], scalar2=None, op0=ALU.mult)
             nc.sync.dma_start(out=out_1[s, i * P:(i + 1) * P, :], in_=lf[:])
 
-        def call(f, *a):
-            return lambda: f(*a)
+        def w_both(m, g, d, k=2):
+            w_copy(m, g, d, range(k), "v")
+            w_copy(m, g, d, range(k, 4), "s")
 
-        def proj(m, s, g):
-            for t in range(4):
-                shift(m, s, g, t, project(m, s, g, t))
-
-        x_mul(0, 0)
-        w_turn(DEP, 0, 0, "vvss")
-        x_turn(0, 0)
-        x_mul(0, 1)
-        x_mul(0, 2)
-        w_quant(DEP, 0, 0)
-        x_turn(0, 1)
-        x_turn(0, 2)
-        w_turn(DEP, 0, 1, "vvss")
-        x_quant(0)
-        w_quant(DEP, 0, 1)
-        x_mul(1, 0)
-        load_vectors()
-        proj(DEP, 0, 0)
-        tasks = [(s, g, m) for s in range(B) for g in range(2) for m in (DEP, HEAD)]
-        for n, (s, g, m) in enumerate(tasks):
-            if n + 1 < len(tasks):
-                s1, g1, m1 = tasks[n + 1]
-                if s1 == 0:
-                    for d in range(2):
-                        w_turn(m1, g1, d, "vvss")
-                        w_quant(m1, g1, d)
-                proj(m1, s1, g1)
-            kink(m, s, g)
-            if n >= 1:
-                s0, g0, m0 = tasks[n - 1]
-                quant(m0, s0, g0)
-            inter(m, s, g)
-            k = n % 4
-            nxt = s + 1
-            if k == 0 and s >= 1:
-                for i in range(NB):
-                    score_mm(s - 1, i)
-            if k == 1 and s >= 1:
-                for i in range(NB):
-                    score_v(s - 1, i)
-                for i in range(NB):
-                    score_e(s - 1, i)
-            if k == 2 and s >= 1:
-                for i in range(NB):
-                    score_l(s - 1, i)
-            if nxt < B:
-                if k == 0:
-                    x_turn(nxt, 0)
-                    x_mul(nxt, 1)
-                if k == 1:
-                    x_turn(nxt, 1)
-                    x_mul(nxt, 2)
-                if k == 2:
-                    x_turn(nxt, 2)
-                    x_quant(nxt)
-                    if nxt + 1 < B:
-                        x_mul(nxt + 1, 0)
-        s0, g0, m0 = tasks[-1]
-        quant(m0, s0, g0)
-        s = B - 1
-        for i in range(NB):
-            score_mm(s, i)
-        for i in range(NB):
-            score_v(s, i)
-            score_e(s, i)
-        for i in range(NB):
-            score_l(s, i)
+        for tok in TPL["pro"]:
+            k, a = tok[:1], tok[1:]
+            if k == "m":
+                x_mul(int(a[0]), int(a[1]), a[2:])
+            elif k == "t":
+                x_turn(0, int(a))
+            elif k == "c":
+                m, d, e = (DEP if a[0] == "D" else HEAD), int(a[1]), a[2]
+                kk = WP[tok[1:3]]
+                w_copy(m, 0, d, range(kk) if e == "v" else range(kk, 4), e)
+            elif k == "q":
+                w_quant(DEP if a[0] == "D" else HEAD, 0, int(a[1]))
+            elif tok == "xq":
+                x_quant(0)
+            elif tok == "lv":
+                load_vectors()
+            elif k == "D":
+                banks[DEP, 0, 0, int(a)] = project(DEP, 0, 0, int(a))
+            elif k == "S":
+                dep_s(0, 0, int(a))
+            elif k == "K":
+                dep_v(0, 0, int(a))
+            else:
+                raise ValueError(tok)
+        pairs = [(s, g) for s in range(B) for g in range(2)]
+        todo, maxed, exped, reced = [], [], [], []
+        for n, (s, g) in enumerate(pairs):
+            lastn = n + 1 == len(pairs)
+            s1, g1 = (None, None) if lastn else pairs[n + 1]
+            lst = TPL["first" if n == 0 else "last" if lastn else "g%d" % g]
+            for tok in lst:
+                k, a = tok[:1], tok[1:]
+                if k == "H":
+                    banks[HEAD, s, g, int(a)] = project(HEAD, s, g, int(a))
+                elif k == "D":
+                    if not lastn:
+                        banks[DEP, s1, g1, int(a)] = project(DEP, s1, g1, int(a))
+                elif k == "Z":
+                    head_s(s, g, int(a))
+                elif k == "S":
+                    if not lastn:
+                        dep_s(s1, g1, int(a))
+                elif k == "K":
+                    if not lastn:
+                        dep_v(s1, g1, int(a))
+                elif k == "X":
+                    sx = s + 2 if a == "0" else s + 1
+                    if sx < B:
+                        x_mul(sx, int(a))
+                elif k == "T":
+                    if s + 1 < B:
+                        x_turn(s + 1, int(a))
+                elif tok == "xq":
+                    if s + 1 < B:
+                        x_quant(s + 1)
+                elif tok == "L":
+                    head_v(s, g)
+                elif tok == "I":
+                    dep_i(s, g)
+                elif tok == "qh":
+                    quant(HEAD, s, g)
+                elif tok == "qd":
+                    quant(DEP, s, g)
+                elif tok == "st":
+                    if s > 0:
+                        for i in range(NB):
+                            score_mm(s - 1, i)
+                        todo = [(s - 1, i) for i in range(NB)]
+                elif tok == "sc":
+                    if todo:
+                        c = todo.pop(0)
+                        score_v(*c)
+                        score_m(*c)
+                        maxed.append(c)
+                elif tok == "ex":
+                    if maxed:
+                        c = maxed.pop(0)
+                        score_e(*c)
+                        exped.append(c)
+                elif tok == "rc":
+                    if exped:
+                        c = exped.pop(0)
+                        score_r(*c)
+                        reced.append(c)
+                elif tok in ("lf", "lg"):
+                    if reced:
+                        c = reced.pop(0)
+                        score_l(*c, "s" if tok == "lf" else "g")
+                elif k == "w":
+                    m = DEP if a[0] == "d" else HEAD
+                    d = int(a[1])
+                    if a[2] == "c":
+                        w_both(m, 1, d, WK[m])
+                    else:
+                        w_quant(m, 1, d)
+                else:
+                    raise ValueError(tok)
+        last = {}
+        for tok in TPL["tail"]:
+            k, a = tok[:2], tok[2:]
+            if k == "mm":
+                score_mm(B - 1, int(a))
+            elif k == "sc":
+                if a:
+                    score_v(B - 1, int(a))
+                elif todo:
+                    c = todo.pop(0)
+                    score_v(*c)
+                    score_m(*c)
+                    maxed.append(c)
+            elif k == "mx":
+                score_m(B - 1, int(a))
+            elif k == "ex":
+                if a:
+                    score_e(B - 1, int(a))
+                elif maxed:
+                    c = maxed.pop(0)
+                    score_e(*c)
+                    exped.append(c)
+            elif k == "rc":
+                if a:
+                    score_r(B - 1, int(a))
+                elif exped:
+                    c = exped.pop(0)
+                    score_r(*c)
+                    reced.append(c)
+            elif k == "lf":
+                if len(a) > 1:
+                    score_l(B - 1, int(a[0]), a[1])
+                elif reced:
+                    score_l(*reced.pop(0), a)
+            else:
+                raise ValueError(tok)
+        if todo or maxed or exped or reced:
+            raise ValueError("left %s %s %s %s" % (todo, maxed, exped, reced))

from contextlib import ExitStack
from functools import partial

import concourse.mybir as mybir
from concourse.masks import make_identity

B, L, D, R = 4, 384, 1024, 1024
FLOPS = 2 * B * L * D * (2 * R) + 2 * B * L * L * R

F32 = mybir.dt.float32
BF16 = mybir.dt.bfloat16
U32 = mybir.dt.uint32
U8 = mybir.dt.uint8
E4M3 = mybir.dt.float8_e4m3fn
X4 = mybir.dt.float8_e4m3fn_x4
ALU = mybir.AluOpType
ACT = mybir.ActivationFunctionType
AX = mybir.AxisListType

P = 128
NB = L // P
SPLIT = ((0, 256), (256, 384))
DEP, HEAD = 0, 1
SLOPE = 0.1
MANUAL = True
ON_V = set()
ON_G = set()
VM = set()
WE = "vvss"
AFF = "gggg"
TPL = {
    "g0": "H0 Z0 H1 H2 Z1 H3 D0 X1 Z2 D2 S0 D1 Z3 S1 lg D3 X2 S2 ex T0 rc K0 T1 L T2 K1 st S3 K3 rc I K2 ex sc qh qd lf sc".split(),
    "g1": "H2 rc H3 X0 H0 lf xq Z0 H1 ex Z3 Z1 rc Z2 lg D0 ex L S0 D1 K0 D2 S1 D3 S2 S3 K1 K2 K3 I sc qh qd".split(),
    "first": "wd0c H2 H3 H1 X1 wd0q H0 wd1c Z0 Z1 Z2 Z3 wh0c wh1c wd1q D1 D0 L D3 S0 S3 S1 D2 T0 X2 S2 I K0 wh0q T2 T1 K1 wh1q K2 K3 qh qd".split(),
    "last": "H0 Z0 H1 rc Z1 H3 I H2 Z3 sc Z2 qd ex ex lf L qh rc lf".split(),
    "pro": "cD0s m00b m00a cD0v t0 m01 m02 cD1s t1 qD0 cH0s cD1v t2 cH1v lv qD1 cH1s xq m10 D0 qH1 D1 S0 K0 S1 D2 D3 cH0v S2 K2 qH0 S3 K1 K3".split(),
    "tail": "mm0 mm1 rc sc0 mm2 sc1 ex mx0 mx1 ex0 sc2 rc ex1 lfv mx2 rc0 lfv rc1 sc ex2 rc ex lfv lf0v lf1v rc2 lfv lfv rc rc lf2v".split(),
}
WK = (0, 2)
WP = {"D0":2,"D1":2,"H0":3,"H1":1}
PF = True
HS = True
LG = "v"


def tile_biaffine_arc_scores_f5_kernel(tc, x_bytes, x_scale, w_dep, b_dep, w_head, b_head, u, v, pos, out_0, out_1):
    nc = tc.nc
    with ExitStack() as ctx:
        keep = ctx.enter_context(tc.tile_pool(name="keep", bufs=1))
        raws = ctx.enter_context(tc.tile_pool(name="raws", bufs=8))
        wgs = ctx.enter_context(tc.tile_pool(name="wgs", bufs=4))
        xbs = ctx.enter_context(tc.tile_pool(name="xbs", bufs=4))
        xgs = ctx.enter_context(tc.tile_pool(name="xgs", bufs=2))
        zs = ctx.enter_context(tc.tile_pool(name="zs", bufs=3))
        ks = ctx.enter_context(tc.tile_pool(name="ks", bufs=2))
        gs = ctx.enter_context(tc.tile_pool(name="gs", bufs=3))
        cods = ctx.enter_context(tc.tile_pool(name="cods", bufs=2))
        soft = ctx.enter_context(tc.tile_pool(name="soft", bufs=6))
        ps1 = ctx.enter_context(tc.psum_pool(name="ps1", bufs=5))
        ps2 = ctx.enter_context(tc.psum_pool(name="ps2", bufs=3))
        if MANUAL:
            ctx.enter_context(tc.manual_schedule())

        ident_f = keep.tile([P, P], F32, name="ident_f")
        make_identity(nc, ident_f[:])
        ident_b = keep.tile([P, P], BF16, name="ident_b")
        nc.gpsimd.tensor_copy(out=ident_b[:], in_=ident_f[:])
        vrow = keep.tile([P, P], BF16, name="vrow")
        nc.vector.memset(vrow[:], 0.0)
        scl = keep.tile([P, D], F32, name="scl")
        for h in range(2):
            nc.scalar.dma_start(out=scl[:, h * 512:(h + 1) * 512], in_=x_scale[:, h * 512:(h + 1) * 512].rearrange("o k -> (o k)").partition_broadcast(P))
        xby = {}

        def x_load(s, b0, b1):
            xbyt = keep.tile([P, b1 - b0, D], U8, name="xbyt%d%d" % (s, b0))
            nc.sync.dma_start(out=xbyt[:], in_=x_bytes[s * L + b0 * P:s * L + b1 * P, :].rearrange("(b p) k -> p b k", p=P))
            for b in range(b0, b1):
                xby[s, b] = xbyt[:, b - b0, :]

        for i, vec in enumerate((b_dep, b_head, u, v)):
            for g in range(2):
                r = 8 * i + 4 * g
                nc.scalar.dma_start(out=vrow[r:r + 4, :].rearrange("t (b i) -> t b i", i=8), in_=vec[g * 512:(g + 1) * 512].rearrange("(b t i) -> t b i", t=4, i=8))
        w_hbm = (w_dep, w_head)
        raw = {}

        def w_load(m, g, d):
            wr = raws.tile([P, 4, 512], BF16, name="wr", tag="wr", align_bytes=64)
            nc.sync.dma_start(out=wr[:], in_=w_hbm[m][d * 512:(d + 1) * 512, g * 512:(g + 1) * 512].rearrange("(p j) c -> p j c", j=4))
            raw[m, g, d] = wr

        x_load(0, 0, 1)
        w_load(DEP, 0, 0)
        x_load(0, 1, 3)
        w_load(DEP, 0, 1)
        w_load(HEAD, 0, 0)
        w_load(HEAD, 0, 1)
        x_load(1, 0, 3)
        w_load(DEP, 1, 0)
        w_load(DEP, 1, 1)
        w_load(HEAD, 1, 0)
        w_load(HEAD, 1, 1)
        x_load(2, 0, 3)
        x_load(3, 0, 3)
        pos_sb = keep.tile([P, NB, L], BF16, name="pos_sb")
        nc.sync.dma_start(out=pos_sb[:], in_=pos.rearrange("(b p) j -> p b j", p=P))

        vcol = keep.tile([P, 4, 2, 4], F32, name="vcol")
        bd, bh, uu, vv = (vcol[:, i] for i in range(4))
        bd_s = keep.tile([P, 2, 4], F32, name="bd_s")
        warm = keep.tile([P, 1], F32, name="warm")
        nc.vector.memset(warm[:], 0.0)
        nc.scalar.activation(out=warm[:], in_=warm[:], func=ACT.Exp)

        def load_vectors():
            bank = ps2.tile([P, P], BF16, name="vbank", tag="aux")
            nc.tensor.transpose(bank[:], vrow[:], ident_b[:])
            nc.vector.tensor_copy(out=vcol[:].rearrange("p i g t -> p (i g t)"), in_=bank[:, 0:32])
            nc.gpsimd.tensor_scalar(out=bd_s[:], in0=bd, scalar1=SLOPE, scalar2=None, op0=ALU.mult)

        w_codes, w_scales = {}, {}

        w_grp = {}

        def w_copy(m, g, d, slots, engine):
            if (m, g, d) not in w_grp:
                w_grp[m, g, d] = wgs.tile([P, 2048], BF16, name="wg", tag="wg", align_bytes=64)
            view = raw[m, g, d][:].rearrange("p j (b t i) -> p t b i j", t=4, i=8)
            out = w_grp[m, g, d][:].rearrange("p (t b i j) -> p t b i j", t=4, i=8, j=4)
            for t in slots:
                if engine == "s":
                    nc.scalar.copy(out=out[:, t], in_=view[:, t])
                else:
                    nc.vector.tensor_copy(out=out[:, t], in_=view[:, t])

        def w_quant(m, g, d):
            wc = keep.tile([P, 512], U32, name="wc%d%d%d" % (m, g, d), align_bytes=64)
            ws = keep.tile([P, 512], U8, name="ws%d%d%d" % (m, g, d), align_bytes=64)
            nc.vector.quantize_mx(out=wc[:].bitcast(X4), scales=ws[:], in_=w_grp[m, g, d][:])
            w_codes[m, g, d], w_scales[m, g, d] = wc, ws

        x_bf, x_grp, x_codes, x_scales = {}, {}, {}, {}

        def x_mul(s, b, half=""):
            if (s, b) not in x_bf:
                x_bf[s, b] = xbs.tile([P, D], BF16, name="xb", tag="xb", align_bytes=64)
            for h in ((0, 1024),) if half == "" else (((0, 512),) if half == "a" else ((512, 1024),)):
                nc.vector.tensor_tensor(out=x_bf[s, b][:, h[0]:h[1]], in0=xby[s, b][:, h[0]:h[1]].bitcast(E4M3), in1=scl[:, h[0]:h[1]], op=ALU.mult)

        def x_turn(s, b):
            if b == 0:
                x_grp[s] = xgs.tile([P, 2, L, 2], F32, name="xg", tag="xg", align_bytes=64)
            words = x_bf[s, b][:].bitcast(F32)
            bank = ps2.tile([P, 2, 2, P], F32, name="xbank", tag="aux")
            for d in range(2):
                for w in range(2):
                    nc.tensor.transpose(bank[:, d, w, :], words[:, 256 * d + w:256 * (d + 1):2], ident_f[:])
            nc.scalar.copy(out=x_grp[s][:, :, b * P:(b + 1) * P, :], in_=bank[:].rearrange("p d w r -> p d r w"))

        def x_quant(s):
            xc = cods.tile([P, 2 * L], U32, name="xc", tag="xc", align_bytes=64)
            xs = cods.tile([P, 2 * L], U8, name="xs", tag="xs", align_bytes=64)
            flat = x_grp[s][:].rearrange("p d n w -> p (d n w)").bitcast(BF16)
            for a, e in ((0, 512), (512, 768)):
                nc.vector.quantize_mx(out=xc[:, a:e].bitcast(X4), scales=xs[:, a:e], in_=flat[:, 4 * a:4 * e])
            x_codes[s], x_scales[s] = xc, xs

        codes = {}

        def get_codes(m, s):
            if (m, s) not in codes:
                c = cods.tile([P, 2, L], U32, name="c%d" % m, tag="c%d" % m, align_bytes=64)
                sc = cods.tile([P, 2, L], U8, name="s%d" % m, tag="s%d" % m, align_bytes=64)
                codes[m, s] = (c, sc)
            return codes[m, s]

        def project(m, s, g, t):
            bank = ps1.tile([P, L], F32, name="bank1", tag="st1")
            for a, e in SPLIT:
                for d in range(2):
                    nc.tensor.matmul_mx(
                        out=bank[:, a:e],
                        lhsT=w_codes[m, g, d][:, t * P:(t + 1) * P].bitcast(X4),
                        lhsT_scale=w_scales[m, g, d][:, t * P:(t + 1) * P],
                        rhs=x_codes[s][:, d * L + a:d * L + e].bitcast(X4),
                        rhs_scale=x_scales[s][:, d * L + a:d * L + e],
                        start=(d == 0), stop=(d == 1))
            return bank

        z_t, q_t, grp = {}, {}, {}

        banks = {}

        def mm(m, s, g):
            for t in range(4):
                banks[m, s, g, t] = project(m, s, g, t)

        def dep_s(s, g, t):
            if t == 0:
                z_t[DEP, s, g] = zs.tile([P, 4, L], F32, name="zd", tag="zd")
            nc.scalar.activation(out=z_t[DEP, s, g][:, t, :], in_=banks[DEP, s, g, t][:], func=ACT.Identity, bias=bd_s[:, g, t:t + 1], scale=SLOPE)

        def dep_v(s, g, t):
            if t == 0:
                q_t[s, g] = (ks.tile([P, 4, L], F32, name="dp", tag="dp"), ks.tile([P, 4, L], BF16, name="qp", tag="qp"))
            dp, qp = q_t[s, g]
            nc.vector.scalar_tensor_tensor(out=dp[:, t, :], in0=banks[DEP, s, g, t][:], scalar=bd[:, g, t:t + 1], in1=z_t[DEP, s, g][:, t, :], op0=ALU.add, op1=ALU.max)
            nc.gpsimd.tensor_scalar(out=qp[:, t, :], in0=dp[:, t, :], scalar1=uu[:, g, t:t + 1], scalar2=vv[:, g, t:t + 1], op0=ALU.mult, op1=ALU.add)

        def dep_i(s, g):
            gr = gs.tile([P, L, 4], BF16, name="gq", tag="gq", align_bytes=64)
            nc.scalar.copy(out=gr[:], in_=q_t[s, g][1][:].rearrange("p t n -> p n t"))
            grp[DEP, s, g] = gr

        def head_s(s, g, t):
            if t == 0:
                z_t[HEAD, s, g] = zs.tile([P, 4, L], F32, name="zh", tag="zh")
            nc.scalar.activation(out=z_t[HEAD, s, g][:, t, :], in_=banks[HEAD, s, g, t][:], func=ACT.Identity, bias=bh[:, g, t:t + 1], scale=1.0)

        def head_v(s, g):
            gr = gs.tile([P, L, 4], BF16, name="gh", tag="gh", align_bytes=64)
            zz = z_t[HEAD, s, g][:].rearrange("p t n -> p n t")
            nc.vector.scalar_tensor_tensor(out=gr[:], in0=zz, scalar=SLOPE, in1=zz, op0=ALU.mult, op1=ALU.max)
            grp[HEAD, s, g] = gr

        def quant(m, s, g):
            c, sc = get_codes(m, s)
            flat = grp[m, s, g][:].rearrange("p n t -> p (n t)")
            for a, e in SPLIT:
                nc.vector.quantize_mx(out=c[:, g, a:e].bitcast(X4), scales=sc[:, g, a:e], in_=flat[:, 4 * a:4 * e])

        sbank, s_sc, s_mx, s_ex, s_sm, s_rc = {}, {}, {}, {}, {}, {}

        def score_mm(s, i):
            (qc, qs), (hc, hs) = codes[DEP, s], codes[HEAD, s]
            bank = ps2.tile([P, L], F32, name="sbank", tag="aux")
            for a, e in SPLIT:
                for g in range(2):
                    nc.tensor.matmul_mx(
                        out=bank[:, a:e],
                        lhsT=qc[:, g, i * P:(i + 1) * P].bitcast(X4), lhsT_scale=qs[:, g, i * P:(i + 1) * P],
                        rhs=hc[:, g, a:e].bitcast(X4), rhs_scale=hs[:, g, a:e],
                        start=(g == 0), stop=(g == 1))
            sbank[s, i] = bank

        def score_v(s, i):
            sc = soft.tile([P, L], F32, name="sc", tag="sc")
            nc.vector.scalar_tensor_tensor(out=sc[:], in0=sbank[s, i][:], scalar=1.0 / 32.0, in1=pos_sb[:, i, :], op0=ALU.mult, op1=ALU.add)
            nc.sync.dma_start(out=out_0[s, i * P:(i + 1) * P, :], in_=sc[:])
            s_sc[s, i] = sc

        def score_m(s, i):
            mx = soft.tile([P, 1], F32, name="mx", tag="mx")
            nc.vector.tensor_reduce(out=mx[:], in_=s_sc[s, i][:], axis=AX.X, op=ALU.max, negate=True)
            s_mx[s, i] = mx

        def score_e(s, i):
            sc, mx = s_sc[s, i], s_mx[s, i]
            ex = soft.tile([P, L], F32, name="ex", tag="ex")
            sm = soft.tile([P, 1], F32, name="sm", tag="sm")
            nc.scalar.activation(out=ex[:], in_=sc[:], func=ACT.Exp, bias=mx[:], scale=1.0, accum_out=sm[:])
            nc.gpsimd.tensor_scalar(out=sm[:], in0=sm[:], scalar1=1.0 / L, scalar2=None, op0=ALU.mult)
            s_ex[s, i], s_sm[s, i] = ex, sm

        def score_r(s, i):
            sm = s_sm[s, i]
            rc = soft.tile([P, 1], F32, name="rc", tag="rc")
            nc.vector.reciprocal(out=rc[:], in_=sm[:])
            s_rc[s, i] = rc

        def score_l(s, i, engine):
            ex, rc = s_ex[s, i], s_rc[s, i]
            lf = soft.tile([P, L], F32, name="lf", tag="lf")
            if engine == "s":
                nc.scalar.activation(out=lf[:], in_=ex[:], func=ACT.Copy, scale=rc[:])
            elif engine == "g":
                nc.gpsimd.tensor_scalar(out=lf[:], in0=ex[:], scalar1=rc[:], scalar2=1.0, op0=ALU.mult, op1=ALU.mult)
            else:
                nc.vector.tensor_scalar(out=lf[:], in0=ex[:], scalar1=rc[:], scalar2=None, op0=ALU.mult)
            nc.sync.dma_start(out=out_1[s, i * P:(i + 1) * P, :], in_=lf[:])

        def w_both(m, g, d, k=2):
            w_copy(m, g, d, range(k), "v")
            w_copy(m, g, d, range(k, 4), "s")

        for tok in TPL["pro"]:
            k, a = tok[:1], tok[1:]
            if k == "m":
                x_mul(int(a[0]), int(a[1]), a[2:])
            elif k == "t":
                x_turn(0, int(a))
            elif k == "c":
                m, d, e = (DEP if a[0] == "D" else HEAD), int(a[1]), a[2]
                kk = WP[tok[1:3]]
                w_copy(m, 0, d, range(kk) if e == "v" else range(kk, 4), e)
            elif k == "q":
                w_quant(DEP if a[0] == "D" else HEAD, 0, int(a[1]))
            elif tok == "xq":
                x_quant(0)
            elif tok == "lv":
                load_vectors()
            elif k == "D":
                banks[DEP, 0, 0, int(a)] = project(DEP, 0, 0, int(a))
            elif k == "S":
                dep_s(0, 0, int(a))
            elif k == "K":
                dep_v(0, 0, int(a))
            else:
                raise ValueError(tok)
        pairs = [(s, g) for s in range(B) for g in range(2)]
        todo, maxed, exped, reced = [], [], [], []
        for n, (s, g) in enumerate(pairs):
            lastn = n + 1 == len(pairs)
            s1, g1 = (None, None) if lastn else pairs[n + 1]
            lst = TPL["first" if n == 0 else "last" if lastn else "g%d" % g]
            for tok in lst:
                k, a = tok[:1], tok[1:]
                if k == "H":
                    banks[HEAD, s, g, int(a)] = project(HEAD, s, g, int(a))
                elif k == "D":
                    if not lastn:
                        banks[DEP, s1, g1, int(a)] = project(DEP, s1, g1, int(a))
                elif k == "Z":
                    head_s(s, g, int(a))
                elif k == "S":
                    if not lastn:
                        dep_s(s1, g1, int(a))
                elif k == "K":
                    if not lastn:
                        dep_v(s1, g1, int(a))
                elif k == "X":
                    sx = s + 2 if a == "0" else s + 1
                    if sx < B:
                        x_mul(sx, int(a))
                elif k == "T":
                    if s + 1 < B:
                        x_turn(s + 1, int(a))
                elif tok == "xq":
                    if s + 1 < B:
                        x_quant(s + 1)
                elif tok == "L":
                    head_v(s, g)
                elif tok == "I":
                    dep_i(s, g)
                elif tok == "qh":
                    quant(HEAD, s, g)
                elif tok == "qd":
                    quant(DEP, s, g)
                elif tok == "st":
                    if s > 0:
                        for i in range(NB):
                            score_mm(s - 1, i)
                        todo = [(s - 1, i) for i in range(NB)]
                elif tok == "sc":
                    if todo:
                        c = todo.pop(0)
                        score_v(*c)
                        score_m(*c)
                        maxed.append(c)
                elif tok == "ex":
                    if maxed:
                        c = maxed.pop(0)
                        score_e(*c)
                        exped.append(c)
                elif tok == "rc":
                    if exped:
                        c = exped.pop(0)
                        score_r(*c)
                        reced.append(c)
                elif tok in ("lf", "lg"):
                    if reced:
                        c = reced.pop(0)
                        score_l(*c, "s" if tok == "lf" else "g")
                elif k == "w":
                    m = DEP if a[0] == "d" else HEAD
                    d = int(a[1])
                    if a[2] == "c":
                        w_both(m, 1, d, WK[m])
                    else:
                        w_quant(m, 1, d)
                else:
                    raise ValueError(tok)
        last = {}
        for tok in TPL["tail"]:
            k, a = tok[:2], tok[2:]
            if k == "mm":
                score_mm(B - 1, int(a))
            elif k == "sc":
                if a:
                    score_v(B - 1, int(a))
                elif todo:
                    c = todo.pop(0)
                    score_v(*c)
                    score_m(*c)
                    maxed.append(c)
            elif k == "mx":
                score_m(B - 1, int(a))
            elif k == "ex":
                if a:
                    score_e(B - 1, int(a))
                elif maxed:
                    c = maxed.pop(0)
                    score_e(*c)
                    exped.append(c)
            elif k == "rc":
                if a:
                    score_r(B - 1, int(a))
                elif exped:
                    c = exped.pop(0)
                    score_r(*c)
                    reced.append(c)
            elif k == "lf":
                if len(a) > 1:
                    score_l(B - 1, int(a[0]), a[1])
                elif reced:
                    score_l(*reced.pop(0), a)
            else:
                raise ValueError(tok)
        if todo or maxed or exped or reced:
            raise ValueError("left %s %s %s %s" % (todo, maxed, exped, reced))
